import numpy as np
import ml_dtypes


def mxq(x, axis, fmt="e4m3"):
    dtype, down = {"e4m3": (ml_dtypes.float8_e4m3fn, 7), "e5m2": (ml_dtypes.float8_e5m2, 14)}[fmt]
    v = np.moveaxis(np.asarray(x, np.float32).astype(ml_dtypes.bfloat16).astype(np.float64), axis, -1)
    blocks = v.reshape(v.shape[:-1] + (-1, 32))
    amax = np.abs(blocks).max(-1, keepdims=True)
    byte = np.maximum(np.where(amax > 0, np.frexp(amax)[1] - 1 + 127, 0) - down, 1)
    scale = np.exp2(byte - 127.0)
    codes = (blocks / scale).astype(np.float32).astype(dtype).astype(np.float64)
    return np.moveaxis((codes * scale).reshape(v.shape), -1, axis)


WIDE = False


def mx_kscale(k):
    if not WIDE:
        return np.ones(k)
    levels = np.array([10, -10, 5, -5, 0])
    if k % 512:
        return np.exp2(np.random.permutation(np.resize(levels, k // 32))).repeat(32)
    a = np.empty((k // 512, 16))
    for p in range(k // 512):
        a[p, :8] = np.random.permutation(np.resize(levels, 8))
        for g in range(8):
            far = levels[np.abs(levels - a[p, g]) >= 10]
            a[p, g + 8] = far[np.random.randint(len(far))]
    return np.exp2(a.ravel()).repeat(32)


def f64(x):
    return np.asarray(x).astype(np.float64)


def striped(idx):
    return np.tile(np.asarray(idx).reshape(-1, 16).T, (8, 1)).astype(np.uint16)


def unstriped(offs):
    return offs[:16].T.reshape(-1).astype(np.int64)


def striped8(idx):
    return np.asarray(idx).reshape(8, -1, 16).transpose(0, 2, 1).reshape(128, -1).astype(np.uint16)


def unstriped8(offs):
    return offs.reshape(8, 16, -1).transpose(0, 2, 1).reshape(8, -1).astype(np.int64)


def pick8(x, idx, run):
    r = np.arange(len(x))
    return x[r[:, None], idx[r % (8 * run) // run]]


E2M1 = np.array([0.0, 0.5, 1.0, 1.5, 2.0, 3.0, 4.0, 6.0, -0.0, -0.5, -1.0, -1.5, -2.0, -3.0, -4.0, -6.0])


def pack_weight(w, fmt):
    k, n = w.shape
    w = f64(np.asarray(w, np.float32).astype(ml_dtypes.bfloat16)).reshape(k // 32, 32, n)
    amax = np.abs(w).max(1)
    if fmt == "e4m3":
        byte = np.frexp(amax)[1] - 1 + 127 - 7
    else:
        mant, ex = np.frexp(amax / 6.0)
        byte = np.where(mant > 0.5, ex, ex - 1) + 127
    byte = np.clip(np.where(amax > 0, byte, 1), 1, 254)
    scaled = (w * np.exp2(127.0 - byte)[:, None, :]).reshape(k, n).astype(np.float32)
    by_word = np.ascontiguousarray(scaled.reshape(k // 512, 128, 4, n).transpose(0, 1, 3, 2))
    if fmt == "e4m3":
        words = by_word.astype(ml_dtypes.float8_e4m3fn).view(np.uint8)
    else:
        c = by_word.astype(ml_dtypes.float4_e2m1fn).view(np.uint8) & 0xF
        words = (c[..., 0::2] | (c[..., 1::2] << 4)).reshape(k // 512, 128, 2 * n)
    return np.ascontiguousarray(words), np.ascontiguousarray(byte.astype(np.uint8).reshape(k // 512, 16, n))


def unpack_weight(words, scales, fmt):
    g, _, n = scales.shape
    words = np.ascontiguousarray(words).reshape(g, 128, n, -1)
    if fmt == "e4m3":
        vals = words.view(ml_dtypes.float8_e4m3fn).astype(np.float64)
    else:
        nib = np.empty((g, 128, n, 4), np.uint8)
        nib[..., 0::2] = words & 0xF
        nib[..., 1::2] = words >> 4
        vals = E2M1[nib]
    vals = vals * np.repeat(np.exp2(scales.astype(np.float64) - 127.0), 8, axis=1)[..., None]
    return vals.transpose(0, 1, 3, 2).reshape(g * 512, n)


K, J, R, T, U, F, C, O, S, N = 512, 256, 512, 1024, 512, 1024, 512, 128, 256, 256


def setup_inputs():
    n = np.random.standard_normal
    idx = np.stack([np.random.permutation(T)[:U] for _ in range(8)])
    idx2 = np.random.permutation(U)[:J]
    idx3 = np.random.permutation(F)[:R]
    idx4 = np.stack([np.random.permutation(C)[:J] for _ in range(8)])
    idx5 = np.stack([np.random.permutation(C)[:S] for _ in range(8)])
    idx6 = np.random.permutation(C)[:S]
    idx7 = np.stack([np.random.permutation(S)[:O] for _ in range(8)])
    fk = mx_kscale(K)
    fr = mx_kscale(R)
    tr = np.ones(F)
    tr[idx3] = fr
    wtp = pack_weight(n((K, F)) * 1 / np.sqrt(K) / fk[:, None] * tr, "e4m3")
    wbp = pack_weight(n((R, N)) * 1 / np.sqrt(R) / fr[:, None], "e2m1")
    return {
        "ta": (np.random.randint(-7, 8, (K, T)).astype(np.float64)).astype(np.float32),
        "ga": ((np.random.randint(8, 25, (K, 1)) / 64.0) * fk[:, None]).astype(np.float32),
        "gb": (np.random.uniform(0.5, 1.6, (K, 1))).astype(np.float32),
        "wt_words": wtp[0],
        "wt_scales": wtp[1],
        "sa": (np.random.uniform(0.5, 1.6, (R, 1))).astype(np.float32),
        "sb": (np.random.uniform(0.5, 1.6, (R, 1))).astype(np.float32),
        "sd": (np.random.uniform(0.5, 1.6, (R, 1))).astype(np.float32),
        "wb_words": wbp[0],
        "wb_scales": wbp[1],
        "offs": striped8(idx),
        "offs2": striped(idx2),
        "offs3": striped(idx3),
        "offs4": striped8(idx4),
        "offs5": striped8(idx5),
        "offs6": striped(idx6),
        "offs7": striped8(idx7),
    }


def reference(ta, ga, gb, wt_words, wt_scales, sa, sb, sd, wb_words, wb_scales, offs, offs2, offs3, offs4, offs5, offs6, offs7):
    idx = unstriped8(offs)
    idx2 = unstriped(offs2)
    idx3 = unstriped(offs3)
    idx4 = unstriped8(offs4)
    idx5 = unstriped8(offs5)
    idx6 = unstriped(offs6)
    idx7 = unstriped8(offs7)
    wtu = unpack_weight(wt_words, wt_scales, "e4m3")
    wbu = unpack_weight(wb_words, wb_scales, "e2m1")
    xcd = pick8(f64(ta), idx, 64) * f64(ga)
    xc = xcd[:, idx2] * f64(gb)
    wtidx3g = wtu[:, idx3]
    xcq = mxq(xc, 0, "e4m3")
    a = wtidx3g.T @ xcq
    pw = np.zeros((R, C))
    pw[np.arange(R)[:, None], idx4[np.arange(R) % 512 // 64]] = a
    pg = np.maximum(pick8(pw, idx5, 64) * f64(sa), pw[:, idx6] * f64(sb))
    hid = pick8(pg, idx7, 64) * f64(sd)
    hidq = mxq(hid, 0, "e4m3")
    y = wbu.T @ hidq
    return y

@@ -1,0 +1,179 @@
+from contextlib import ExitStack
+
+import concourse.mybir as mybir
+
+K, J, R, T, U, F, C, O, S, N = 512, 256, 512, 1024, 512, 1024, 512, 128, 256, 256
+FLOPS = 2 * K * R * J + 2 * R * N * O
+
+F32 = mybir.dt.float32
+BF16 = mybir.dt.bfloat16
+I32 = mybir.dt.int32
+U32 = mybir.dt.uint32
+U16 = mybir.dt.uint16
+U8 = mybir.dt.uint8
+FP8X4 = mybir.dt.float8_e4m3fn_x4
+FP4X4 = mybir.dt.float4_e2m1fn_x4
+COPY = mybir.ActivationFunctionType.Copy
+MAX = mybir.AluOpType.max
+
+P = 128
+PACK = 4
+GROUP = 16
+HALVES = 2
+JH = J // HALVES
+
+
+def tile_picked_respelled_store_one_ladder_one_plain_kernel(
+    tc, ta, ga, gb, wt_words, wt_scales, sa, sb, sd, wb_words, wb_scales,
+    offs, offs2, offs3, offs4, offs5, offs6, offs7, out,
+):
+    nc = tc.nc
+    with ExitStack() as ctx:
+        pool = ctx.enter_context(tc.tile_pool(name="pool", bufs=1))
+        psum = ctx.enter_context(tc.psum_pool(name="psum", bufs=1))
+
+        def load_list(src, name):
+            dst = pool.tile(list(src.shape), U16, name=name)
+            nc.sync.dma_start(dst[:], src)
+            return dst
+
+        def load_factor(queue, src, name):
+            dst = pool.tile([P, PACK], F32, name=name)
+            queue.dma_start(dst[:], src.rearrange("(p t) o -> p (t o)", t=PACK))
+            return dst
+
+        def load_scale_rows(src, name):
+            words = src.shape[2] // 4
+            stage = pool.tile([P, 2, words], I32, name=name)
+            rows = src[0].bitcast(I32).rearrange("(u q i) w -> u i q w", u=2, q=2)
+            for u in range(2):
+                nc.sync.dma_start(stage[64 * u : 64 * u + 4], rows[u])
+            return stage
+
+        def spread_scale_rows(stage, plane):
+            for u in range(2):
+                for q in range(2):
+                    first = 64 * u + 32 * q
+                    nc.vector.tensor_copy(plane[first : first + 4, :].bitcast(I32), stage[64 * u : 64 * u + 4, q, :])
+
+        def interleave(planes, width, name):
+            grouped = pool.tile([P, width, PACK], BF16, name=name, align_bytes=64)
+            nc.vector.tensor_copy(
+                grouped[:].rearrange("p (c i) t -> p c t i", i=4),
+                planes[:].rearrange("p t (c i) -> p c t i", i=4),
+            )
+            return grouped
+
+        def quantize(grouped, width, name):
+            codes = pool.tile([P, width], U32, name=name + "_codes", align_bytes=64)
+            scales = pool.tile([P, width], U8, name=name + "_scales", align_bytes=64)
+            nc.vector.quantize_mx(
+                out=codes[:].bitcast(FP8X4), scales=scales[:], in_=grouped[:].rearrange("p c t -> p (c t)")
+            )
+            return codes, scales
+
+        ta_rows = ta.rearrange("(p t) c -> t p c", t=PACK)
+        ta_sb = [pool.tile([P, T], F32, name="ta%d" % t) for t in range(PACK)]
+
+        nc.sync.dma_start(ta_sb[0][:], ta_rows[0])
+        l1 = load_list(offs, "l1")
+        ga_sb = load_factor(nc.scalar, ga, "ga_sb")
+        gb_sb = load_factor(nc.scalar, gb, "gb_sb")
+        l2 = load_list(offs2, "l2")
+        nc.sync.dma_start(ta_sb[1][:], ta_rows[1])
+        wt_stage = load_scale_rows(wt_scales, "wt_stage")
+        nc.sync.dma_start(ta_sb[2][:], ta_rows[2])
+        l3 = load_list(offs3, "l3")
+        wt_store = pool.tile([P, F], U32, name="wt_store")
+        nc.sync.dma_start(wt_store[:].bitcast(I32), wt_words[0].rearrange("p f t -> p (f t)").bitcast(I32))
+        nc.sync.dma_start(ta_sb[3][:], ta_rows[3])
+        l4 = load_list(offs4, "l4")
+        l5 = load_list(offs5, "l5")
+        l6 = load_list(offs6, "l6")
+        sa_sb = load_factor(nc.sync, sa, "sa_sb")
+        sb_sb = load_factor(nc.sync, sb, "sb_sb")
+        l7 = load_list(offs7, "l7")
+        sd_sb = load_factor(nc.sync, sd, "sd_sb")
+        wb_stage = load_scale_rows(wb_scales, "wb_stage")
+        wb_codes = pool.tile([P, 2 * N], U8, name="wb_codes", align_bytes=64)
+        nc.sync.dma_start(wb_codes[:].bitcast(I32), wb_words[0].bitcast(I32))
+
+        wt_store_plane = pool.tile([P, F], U8, name="wt_store_plane")
+        nc.vector.memset(wt_store_plane[:].bitcast(I32), 0)
+        pw = [pool.tile([P, C], F32, name="pw%d" % t) for t in range(PACK)]
+        for t in range(PACK):
+            nc.vector.memset(pw[t][:], 0.0)
+        spread_scale_rows(wt_stage, wt_store_plane)
+        wt_plane = pool.tile([P, PACK, P], U8, name="wt_plane", align_bytes=64)
+        nc.vector.tensor_copy(wt_plane[:].rearrange("p t m -> p m t"), wt_store_plane[:].indirect(l3[:]))
+        wt_codes = pool.tile([P, PACK, P], U32, name="wt_codes", align_bytes=64)
+        nc.vector.tensor_copy(wt_codes[:].rearrange("p t m -> p m t"), wt_store[:].indirect(l3[:]))
+
+        xcd = [pool.tile([P, U], F32, name="xcd%d" % t) for t in range(PACK)]
+        xc = [pool.tile([P, PACK, JH], BF16, name="xc0")]
+        half_cols = JH // GROUP
+
+        def read_slots(h, t):
+            nc.scalar.activation(
+                xc[h][:, t, :], xcd[t][:].indirect(l2[:, h * half_cols : (h + 1) * half_cols]), COPY,
+                scale=gb_sb[:, t : t + 1],
+            )
+
+        for t in range(PACK):
+            nc.scalar.activation(xcd[t][:], ta_sb[t][:].indirect(l1[:]), COPY, scale=ga_sb[:, t : t + 1])
+            read_slots(0, t)
+        xc.append(pool.tile([P, PACK, JH], BF16, name="xc1", tag="ta3"))
+        for t in range(PACK):
+            read_slots(1, t)
+
+        a_sb = [pool.tile([P, J], F32, name="a%d" % t) for t in range(PACK)]
+        for h in range(HALVES):
+            grouped = interleave(xc[h], JH, "xg%d" % h)
+            codes, scales = quantize(grouped, JH, "xq%d" % h)
+            for t in range(PACK):
+                acc = psum.tile([P, JH], F32, name="acc%d_%d" % (h, t), tag="acc%d" % t)
+                nc.tensor.matmul_mx(
+                    out=acc[:], lhsT=wt_codes[:, t, :].bitcast(FP8X4), lhsT_scale=wt_plane[:, t, :],
+                    rhs=codes[:].bitcast(FP8X4), rhs_scale=scales[:], start=True, stop=True,
+                )
+                nc.scalar.copy(a_sb[t][:, h * JH : (h + 1) * JH], acc[:])
+
+        for h in range(HALVES):
+            for t in range(2):
+                nc.vector.tensor_copy(
+                    pw[t][:].indirect(l4[:, h * half_cols : (h + 1) * half_cols]), a_sb[t][:, h * JH : (h + 1) * JH]
+                )
+        for t in range(2, PACK):
+            nc.vector.tensor_copy(pw[t][:].indirect(l4[:]), a_sb[t][:])
+
+        wb_plane = pool.tile([P, N], U8, name="wb_plane", align_bytes=64)
+        spread_scale_rows(wb_stage, wb_plane)
+
+        own = [pool.tile([P, S], F32, name="own%d" % t) for t in range(PACK)]
+        shared = [pool.tile([P, S], F32, name="shared%d" % t) for t in range(PACK)]
+        pg = [pool.tile([P, S], F32, name="pg%d" % t) for t in range(PACK)]
+        hid = pool.tile([P, PACK, O], BF16, name="hid")
+        for t in range(PACK):
+            nc.scalar.activation(own[t][:], pw[t][:].indirect(l5[:]), COPY, scale=sa_sb[:, t : t + 1])
+            nc.scalar.activation(shared[t][:], pw[t][:].indirect(l6[:]), COPY, scale=sb_sb[:, t : t + 1])
+        for t in range(PACK):
+            nc.vector.tensor_tensor(pg[t][:], own[t][:], shared[t][:], MAX)
+        for t in range(PACK):
+            nc.scalar.activation(hid[:, t, :], pg[t][:].indirect(l7[:]), COPY, scale=sd_sb[:, t : t + 1])
+
+        grouped = interleave(hid, O, "hg")
+        codes, scales = quantize(grouped, O, "hq")
+        for u in range(N // P):
+            acc = psum.tile([P, O], F32, name="y%d" % u)
+            nc.tensor.matmul_mx(
+                out=acc[:], lhsT=wb_codes[:, 2 * P * u : 2 * P * (u + 1)].bitcast(FP4X4),
+                lhsT_scale=wb_plane[:, P * u : P * (u + 1)],
+                rhs=codes[:].bitcast(FP8X4), rhs_scale=scales[:], start=True, stop=True,
+            )
+            y = pool.tile([P, O], F32, name="y_sb%d" % u)
+            if u == 0:
+                nc.vector.tensor_copy(y[:], acc[:])
+                nc.sync.dma_start(out[P * u : P * (u + 1), :], y[:])
+            else:
+                nc.scalar.copy(y[:], acc[:])
+                nc.scalar.dma_start(out[P * u : P * (u + 1), :], y[:])

@@ -98,6 +98,10 @@ def tile_picked_respelled_store_one_ladder_one_plain_kernel(
         wb_codes = pool.tile([P, 2 * N], U8, name="wb_codes", align_bytes=64)
         nc.sync.dma_start(wb_codes[:].bitcast(I32), wb_words[0].bitcast(I32))
 
+        warm = pool.tile([P, 2], F32, name="warm")
+        nc.gpsimd.memset(warm[:, 0:1], 0.0)
+        nc.scalar.activation(warm[:, 1:2], warm[:, 0:1], COPY)
+
         wt_store_plane = pool.tile([P, F], U8, name="wt_store_plane")
         nc.vector.memset(wt_store_plane[:].bitcast(I32), 0)
         pw = [pool.tile([P, C], F32, name="pw%d" % t) for t in range(PACK)]

@@ -56,13 +56,11 @@ def tile_picked_respelled_store_one_ladder_one_plain_kernel(
                     first = 64 * u + 32 * q
                     nc.vector.tensor_copy(plane[first : first + 4, :].bitcast(I32), stage[64 * u : 64 * u + 4, q, :])
 
-        def interleave(planes, width, name):
-            grouped = pool.tile([P, width, PACK], BF16, name=name, align_bytes=64)
+        def interleave(grouped, planes):
             nc.vector.tensor_copy(
                 grouped[:].rearrange("p (c i) t -> p c t i", i=4),
                 planes[:].rearrange("p t (c i) -> p c t i", i=4),
             )
-            return grouped
 
         def quantize(grouped, width, name):
             codes = pool.tile([P, width], U32, name=name + "_codes", align_bytes=64)
@@ -75,14 +73,14 @@ def tile_picked_respelled_store_one_ladder_one_plain_kernel(
         ta_rows = ta.rearrange("(p t) c -> t p c", t=PACK)
         ta_sb = [pool.tile([P, T], F32, name="ta%d" % t) for t in range(PACK)]
 
-        nc.sync.dma_start(ta_sb[0][:], ta_rows[0])
         l1 = load_list(offs, "l1")
         ga_sb = load_factor(nc.scalar, ga, "ga_sb")
-        gb_sb = load_factor(nc.scalar, gb, "gb_sb")
-        l2 = load_list(offs2, "l2")
+        nc.sync.dma_start(ta_sb[0][:], ta_rows[0])
         nc.sync.dma_start(ta_sb[1][:], ta_rows[1])
         wt_stage = load_scale_rows(wt_scales, "wt_stage")
+        l2 = load_list(offs2, "l2")
         nc.sync.dma_start(ta_sb[2][:], ta_rows[2])
+        gb_sb = load_factor(nc.sync, gb, "gb_sb")
         l3 = load_list(offs3, "l3")
         wt_store = pool.tile([P, F], U32, name="wt_store")
         nc.sync.dma_start(wt_store[:].bitcast(I32), wt_words[0].rearrange("p f t -> p (f t)").bitcast(I32))
@@ -114,7 +112,7 @@ def tile_picked_respelled_store_one_ladder_one_plain_kernel(
         nc.vector.tensor_copy(wt_codes[:].rearrange("p t m -> p m t"), wt_store[:].indirect(l3[:]))
 
         xcd = [pool.tile([P, U], F32, name="xcd%d" % t) for t in range(PACK)]
-        xc = [pool.tile([P, PACK, JH], BF16, name="xc0")]
+        xc = [pool.tile([P, PACK, JH], BF16, name="xc%d" % h, tag="ta%d" % (2 + h)) for h in range(HALVES)]
         half_cols = JH // GROUP
 
         def read_slots(h, t):
@@ -125,14 +123,14 @@ def tile_picked_respelled_store_one_ladder_one_plain_kernel(
 
         for t in range(PACK):
             nc.scalar.activation(xcd[t][:], ta_sb[t][:].indirect(l1[:]), COPY, scale=ga_sb[:, t : t + 1])
-            read_slots(0, t)
-        xc.append(pool.tile([P, PACK, JH], BF16, name="xc1", tag="ta3"))
-        for t in range(PACK):
-            read_slots(1, t)
+        for h in range(HALVES):
+            for t in range(PACK):
+                read_slots(h, t)
 
         a_sb = [pool.tile([P, J], F32, name="a%d" % t) for t in range(PACK)]
         for h in range(HALVES):
-            grouped = interleave(xc[h], JH, "xg%d" % h)
+            grouped = pool.tile([P, JH, PACK], BF16, name="xg%d" % h, align_bytes=64)
+            interleave(grouped, xc[h])
             codes, scales = quantize(grouped, JH, "xq%d" % h)
             for t in range(PACK):
                 acc = psum.tile([P, JH], F32, name="acc%d_%d" % (h, t), tag="acc%d" % t)
@@ -165,7 +163,8 @@ def tile_picked_respelled_store_one_ladder_one_plain_kernel(
         for t in range(PACK):
             nc.scalar.activation(hid[:, t, :], pg[t][:].indirect(l7[:]), COPY, scale=sd_sb[:, t : t + 1])
 
-        grouped = interleave(hid, O, "hg")
+        grouped = pool.tile([P, O, PACK], BF16, name="hg", align_bytes=64)
+        interleave(grouped, hid)
         codes, scales = quantize(grouped, O, "hq")
         for u in range(N // P):
             acc = psum.tile([P, O], F32, name="y%d" % u)

@@ -73,18 +73,21 @@ def tile_picked_respelled_store_one_ladder_one_plain_kernel(
         ta_rows = ta.rearrange("(p t) c -> t p c", t=PACK)
         ta_sb = [pool.tile([P, T], F32, name="ta%d" % t) for t in range(PACK)]
 
+        nc.sync.dma_start(ta_sb[0][:], ta_rows[0])
         l1 = load_list(offs, "l1")
         ga_sb = load_factor(nc.scalar, ga, "ga_sb")
-        nc.sync.dma_start(ta_sb[0][:], ta_rows[0])
+        warm = pool.tile([P, 2], F32, name="warm")
+        nc.gpsimd.memset(warm[:, 0:1], 0.0)
+        nc.scalar.activation(warm[:, 1:2], warm[:, 0:1], COPY)
         nc.sync.dma_start(ta_sb[1][:], ta_rows[1])
         wt_stage = load_scale_rows(wt_scales, "wt_stage")
-        l2 = load_list(offs2, "l2")
-        nc.sync.dma_start(ta_sb[2][:], ta_rows[2])
-        gb_sb = load_factor(nc.sync, gb, "gb_sb")
         l3 = load_list(offs3, "l3")
-        wt_store = pool.tile([P, F], U32, name="wt_store")
-        nc.sync.dma_start(wt_store[:].bitcast(I32), wt_words[0].rearrange("p f t -> p (f t)").bitcast(I32))
+        nc.sync.dma_start(ta_sb[2][:], ta_rows[2])
         nc.sync.dma_start(ta_sb[3][:], ta_rows[3])
+        l2 = load_list(offs2, "l2")
+        gb_sb = load_factor(nc.sync, gb, "gb_sb")
+        wt_store = pool.tile([P, F], U32, name="wt_store", align_bytes=64)
+        nc.sync.dma_start(wt_store[:].bitcast(I32), wt_words[0].rearrange("p f t -> p (f t)").bitcast(I32))
         l4 = load_list(offs4, "l4")
         l5 = load_list(offs5, "l5")
         l6 = load_list(offs6, "l6")
@@ -92,13 +95,13 @@ def tile_picked_respelled_store_one_ladder_one_plain_kernel(
         sb_sb = load_factor(nc.sync, sb, "sb_sb")
         l7 = load_list(offs7, "l7")
         sd_sb = load_factor(nc.sync, sd, "sd_sb")
-        wb_stage = load_scale_rows(wb_scales, "wb_stage")
+        wb_plane = pool.tile([P, N], U8, name="wb_plane", align_bytes=64)
+        for q in range(4):
+            nc.sync.dma_start(
+                wb_plane[32 * q : 32 * q + 4, :].bitcast(I32), wb_scales[0, 4 * q : 4 * q + 4, :].bitcast(I32)
+            )
         wb_codes = pool.tile([P, 2 * N], U8, name="wb_codes", align_bytes=64)
         nc.sync.dma_start(wb_codes[:].bitcast(I32), wb_words[0].bitcast(I32))
-
-        warm = pool.tile([P, 2], F32, name="warm")
-        nc.gpsimd.memset(warm[:, 0:1], 0.0)
-        nc.scalar.activation(warm[:, 1:2], warm[:, 0:1], COPY)
 
         wt_store_plane = pool.tile([P, F], U8, name="wt_store_plane")
         nc.vector.memset(wt_store_plane[:].bitcast(I32), 0)
@@ -112,7 +115,7 @@ def tile_picked_respelled_store_one_ladder_one_plain_kernel(
         nc.vector.tensor_copy(wt_codes[:].rearrange("p t m -> p m t"), wt_store[:].indirect(l3[:]))
 
         xcd = [pool.tile([P, U], F32, name="xcd%d" % t) for t in range(PACK)]
-        xc = [pool.tile([P, PACK, JH], BF16, name="xc%d" % h, tag="ta%d" % (2 + h)) for h in range(HALVES)]
+        xc = [pool.tile([P, PACK, JH], BF16, name="xc%d" % h) for h in range(HALVES)]
         half_cols = JH // GROUP
 
         def read_slots(h, t):
@@ -129,7 +132,7 @@ def tile_picked_respelled_store_one_ladder_one_plain_kernel(
 
         a_sb = [pool.tile([P, J], F32, name="a%d" % t) for t in range(PACK)]
         for h in range(HALVES):
-            grouped = pool.tile([P, JH, PACK], BF16, name="xg%d" % h, align_bytes=64)
+            grouped = pool.tile([P, JH, PACK], BF16, name="xg%d" % h, align_bytes=64, tag="wt_store")
             interleave(grouped, xc[h])
             codes, scales = quantize(grouped, JH, "xq%d" % h)
             for t in range(PACK):
@@ -147,9 +150,6 @@ def tile_picked_respelled_store_one_ladder_one_plain_kernel(
                 )
         for t in range(2, PACK):
             nc.vector.tensor_copy(pw[t][:].indirect(l4[:]), a_sb[t][:])
-
-        wb_plane = pool.tile([P, N], U8, name="wb_plane", align_bytes=64)
-        spread_scale_rows(wb_stage, wb_plane)
 
         own = [pool.tile([P, S], F32, name="own%d" % t) for t in range(PACK)]
         shared = [pool.tile([P, S], F32, name="shared%d" % t) for t in range(PACK)]

from contextlib import ExitStack

import concourse.mybir as mybir

K, J, R, T, U, F, C, O, S, N = 512, 256, 512, 1024, 512, 1024, 512, 128, 256, 256
FLOPS = 2 * K * R * J + 2 * R * N * O

F32 = mybir.dt.float32
BF16 = mybir.dt.bfloat16
I32 = mybir.dt.int32
U32 = mybir.dt.uint32
U16 = mybir.dt.uint16
U8 = mybir.dt.uint8
FP8X4 = mybir.dt.float8_e4m3fn_x4
FP4X4 = mybir.dt.float4_e2m1fn_x4
COPY = mybir.ActivationFunctionType.Copy
MAX = mybir.AluOpType.max

P = 128
PACK = 4
GROUP = 16
HALVES = 2
JH = J // HALVES


def tile_picked_respelled_store_one_ladder_one_plain_kernel(
    tc, ta, ga, gb, wt_words, wt_scales, sa, sb, sd, wb_words, wb_scales,
    offs, offs2, offs3, offs4, offs5, offs6, offs7, out,
):
    nc = tc.nc
    with ExitStack() as ctx:
        pool = ctx.enter_context(tc.tile_pool(name="pool", bufs=1))
        psum = ctx.enter_context(tc.psum_pool(name="psum", bufs=1))

        def load_list(src, name):
            dst = pool.tile(list(src.shape), U16, name=name)
            nc.sync.dma_start(dst[:], src)
            return dst

        def load_factor(queue, src, name):
            dst = pool.tile([P, PACK], F32, name=name)
            queue.dma_start(dst[:], src.rearrange("(p t) o -> p (t o)", t=PACK))
            return dst

        def load_scale_rows(src, name):
            words = src.shape[2] // 4
            stage = pool.tile([P, 2, words], I32, name=name)
            rows = src[0].bitcast(I32).rearrange("(u q i) w -> u i q w", u=2, q=2)
            for u in range(2):
                nc.sync.dma_start(stage[64 * u : 64 * u + 4], rows[u])
            return stage

        def spread_scale_rows(stage, plane):
            for u in range(2):
                for q in range(2):
                    first = 64 * u + 32 * q
                    nc.vector.tensor_copy(plane[first : first + 4, :].bitcast(I32), stage[64 * u : 64 * u + 4, q, :])

        def interleave(grouped, planes):
            nc.vector.tensor_copy(
                grouped[:].rearrange("p (c i) t -> p c t i", i=4),
                planes[:].rearrange("p t (c i) -> p c t i", i=4),
            )

        def quantize(grouped, width, name):
            codes = pool.tile([P, width], U32, name=name + "_codes", align_bytes=64)
            scales = pool.tile([P, width], U8, name=name + "_scales", align_bytes=64)
            nc.vector.quantize_mx(
                out=codes[:].bitcast(FP8X4), scales=scales[:], in_=grouped[:].rearrange("p c t -> p (c t)")
            )
            return codes, scales

        ta_rows = ta.rearrange("(p t) c -> t p c", t=PACK)
        ta_sb = [pool.tile([P, T], F32, name="ta%d" % t) for t in range(PACK)]

        nc.sync.dma_start(ta_sb[0][:], ta_rows[0])
        l1 = load_list(offs, "l1")
        ga_sb = load_factor(nc.scalar, ga, "ga_sb")
        warm = pool.tile([P, 2], F32, name="warm")
        nc.gpsimd.memset(warm[:, 0:1], 0.0)
        nc.scalar.activation(warm[:, 1:2], warm[:, 0:1], COPY)
        nc.sync.dma_start(ta_sb[1][:], ta_rows[1])
        wt_stage = load_scale_rows(wt_scales, "wt_stage")
        l3 = load_list(offs3, "l3")
        nc.sync.dma_start(ta_sb[2][:], ta_rows[2])
        nc.sync.dma_start(ta_sb[3][:], ta_rows[3])
        l2 = load_list(offs2, "l2")
        gb_sb = load_factor(nc.sync, gb, "gb_sb")
        wt_store = pool.tile([P, F], U32, name="wt_store", align_bytes=64)
        nc.sync.dma_start(wt_store[:].bitcast(I32), wt_words[0].rearrange("p f t -> p (f t)").bitcast(I32))
        l4 = load_list(offs4, "l4")
        l5 = load_list(offs5, "l5")
        l6 = load_list(offs6, "l6")
        sa_sb = load_factor(nc.sync, sa, "sa_sb")
        sb_sb = load_factor(nc.sync, sb, "sb_sb")
        l7 = load_list(offs7, "l7")
        sd_sb = load_factor(nc.sync, sd, "sd_sb")
        wb_plane = pool.tile([P, N], U8, name="wb_plane", align_bytes=64)
        for q in range(4):
            nc.sync.dma_start(
                wb_plane[32 * q : 32 * q + 4, :].bitcast(I32), wb_scales[0, 4 * q : 4 * q + 4, :].bitcast(I32)
            )
        wb_codes = pool.tile([P, 2 * N], U8, name="wb_codes", align_bytes=64)
        nc.sync.dma_start(wb_codes[:].bitcast(I32), wb_words[0].bitcast(I32))

        wt_store_plane = pool.tile([P, F], U8, name="wt_store_plane")
        nc.vector.memset(wt_store_plane[:].bitcast(I32), 0)
        pw = [pool.tile([P, C], F32, name="pw%d" % t) for t in range(PACK)]
        for t in range(PACK):
            nc.vector.memset(pw[t][:], 0.0)
        spread_scale_rows(wt_stage, wt_store_plane)
        wt_plane = pool.tile([P, PACK, P], U8, name="wt_plane", align_bytes=64)
        nc.vector.tensor_copy(wt_plane[:].rearrange("p t m -> p m t"), wt_store_plane[:].indirect(l3[:]))
        wt_codes = pool.tile([P, PACK, P], U32, name="wt_codes", align_bytes=64)
        nc.vector.tensor_copy(wt_codes[:].rearrange("p t m -> p m t"), wt_store[:].indirect(l3[:]))

        xcd = [pool.tile([P, U], F32, name="xcd%d" % t) for t in range(PACK)]
        xc = [pool.tile([P, PACK, JH], BF16, name="xc%d" % h) for h in range(HALVES)]
        half_cols = JH // GROUP

        def read_slots(h, t):
            nc.scalar.activation(
                xc[h][:, t, :], xcd[t][:].indirect(l2[:, h * half_cols : (h + 1) * half_cols]), COPY,
                scale=gb_sb[:, t : t + 1],
            )

        for t in range(PACK):
            nc.scalar.activation(xcd[t][:], ta_sb[t][:].indirect(l1[:]), COPY, scale=ga_sb[:, t : t + 1])
        for h in range(HALVES):
            for t in range(PACK):
                read_slots(h, t)

        a_sb = [pool.tile([P, J], F32, name="a%d" % t) for t in range(PACK)]
        for h in range(HALVES):
            grouped = pool.tile([P, JH, PACK], BF16, name="xg%d" % h, align_bytes=64, tag="wt_store")
            interleave(grouped, xc[h])
            codes, scales = quantize(grouped, JH, "xq%d" % h)
            for t in range(PACK):
                acc = psum.tile([P, JH], F32, name="acc%d_%d" % (h, t), tag="acc%d" % t)
                nc.tensor.matmul_mx(
                    out=acc[:], lhsT=wt_codes[:, t, :].bitcast(FP8X4), lhsT_scale=wt_plane[:, t, :],
                    rhs=codes[:].bitcast(FP8X4), rhs_scale=scales[:], start=True, stop=True,
                )
                nc.scalar.copy(a_sb[t][:, h * JH : (h + 1) * JH], acc[:])

        for h in range(HALVES):
            for t in range(2):
                nc.vector.tensor_copy(
                    pw[t][:].indirect(l4[:, h * half_cols : (h + 1) * half_cols]), a_sb[t][:, h * JH : (h + 1) * JH]
                )
        for t in range(2, PACK):
            nc.vector.tensor_copy(pw[t][:].indirect(l4[:]), a_sb[t][:])

        own = [pool.tile([P, S], F32, name="own%d" % t) for t in range(PACK)]
        shared = [pool.tile([P, S], F32, name="shared%d" % t) for t in range(PACK)]
        pg = [pool.tile([P, S], F32, name="pg%d" % t) for t in range(PACK)]
        hid = pool.tile([P, PACK, O], BF16, name="hid")
        for t in range(PACK):
            nc.scalar.activation(own[t][:], pw[t][:].indirect(l5[:]), COPY, scale=sa_sb[:, t : t + 1])
            nc.scalar.activation(shared[t][:], pw[t][:].indirect(l6[:]), COPY, scale=sb_sb[:, t : t + 1])
        for t in range(PACK):
            nc.vector.tensor_tensor(pg[t][:], own[t][:], shared[t][:], MAX)
        for t in range(PACK):
            nc.scalar.activation(hid[:, t, :], pg[t][:].indirect(l7[:]), COPY, scale=sd_sb[:, t : t + 1])

        grouped = pool.tile([P, O, PACK], BF16, name="hg", align_bytes=64)
        interleave(grouped, hid)
        codes, scales = quantize(grouped, O, "hq")
        for u in range(N // P):
            acc = psum.tile([P, O], F32, name="y%d" % u)
            nc.tensor.matmul_mx(
                out=acc[:], lhsT=wb_codes[:, 2 * P * u : 2 * P * (u + 1)].bitcast(FP4X4),
                lhsT_scale=wb_plane[:, P * u : P * (u + 1)],
                rhs=codes[:].bitcast(FP8X4), rhs_scale=scales[:], start=True, stop=True,
            )
            y = pool.tile([P, O], F32, name="y_sb%d" % u)
            if u == 0:
                nc.vector.tensor_copy(y[:], acc[:])
                nc.sync.dma_start(out[P * u : P * (u + 1), :], y[:])
            else:
                nc.scalar.copy(y[:], acc[:])
                nc.scalar.dma_start(out[P * u : P * (u + 1), :], y[:])
